import numpy as np
import ml_dtypes


def mxq(x, axis, fmt="e4m3"):
    dtype, down = {"e4m3": (ml_dtypes.float8_e4m3fn, 7), "e5m2": (ml_dtypes.float8_e5m2, 14)}[fmt]
    v = np.moveaxis(np.asarray(x, np.float32).astype(ml_dtypes.bfloat16).astype(np.float64), axis, -1)
    blocks = v.reshape(v.shape[:-1] + (-1, 32))
    amax = np.abs(blocks).max(-1, keepdims=True)
    byte = np.maximum(np.where(amax > 0, np.frexp(amax)[1] - 1 + 127, 0) - down, 1)
    scale = np.exp2(byte - 127.0)
    codes = (blocks / scale).astype(np.float32).astype(dtype).astype(np.float64)
    return np.moveaxis((codes * scale).reshape(v.shape), -1, axis)


WIDE = False


def mx_kscale(k):
    if not WIDE:
        return np.ones(k)
    levels = np.array([10, -10, 5, -5, 0])
    if k % 512:
        return np.exp2(np.random.permutation(np.resize(levels, k // 32))).repeat(32)
    a = np.empty((k // 512, 16))
    for p in range(k // 512):
        a[p, :8] = np.random.permutation(np.resize(levels, 8))
        for g in range(8):
            far = levels[np.abs(levels - a[p, g]) >= 10]
            a[p, g + 8] = far[np.random.randint(len(far))]
    return np.exp2(a.ravel()).repeat(32)


def f64(x):
    return np.asarray(x).astype(np.float64)


def striped(idx):
    return np.tile(idx.reshape(-1, 16).T, (8, 1)).astype(np.uint16)


def unstriped(offs):
    return offs[:16].T.reshape(-1).astype(np.int64)


def pack_weight(w):
    k, n = w.shape
    w = f64(np.asarray(w, np.float32).astype(ml_dtypes.bfloat16)).reshape(k // 32, 32, n)
    amax = np.abs(w).max(1)
    byte = np.clip(np.where(amax > 0, np.frexp(amax)[1] - 1 + 127 - 7, 1), 1, 254)
    scaled = (w * np.exp2(127.0 - byte)[:, None, :]).reshape(k, n).astype(np.float32)
    words = np.ascontiguousarray(scaled.reshape(k // 512, 128, 4, n).transpose(0, 1, 3, 2)).astype(ml_dtypes.float8_e4m3fn).view(np.uint8)
    return words, np.ascontiguousarray(byte.astype(np.uint8).reshape(k // 512, 16, n))


def unpack_weight(words, scales):
    g, p, n, _ = words.shape
    vals = np.ascontiguousarray(words).view(ml_dtypes.float8_e4m3fn).astype(np.float64) * np.repeat(np.exp2(scales.astype(np.float64) - 127.0), 8, axis=1)[..., None]
    return vals.transpose(0, 1, 3, 2).reshape(g * 512, n)


def gelu(v):
    return 0.5 * v * (1.0 + np.tanh(np.sqrt(2.0 / np.pi) * (v + 0.044715 * v**3)))


K, T, S, N, H, V, U = 1024, 2048, 512, 128, 512, 256, 512


def setup_inputs():
    n = np.random.standard_normal
    s = mx_kscale(K)[:, None]
    u = mx_kscale(H)
    packed_xT = pack_weight(n((K, T)) * s)
    return {
        "x_words": packed_xT[0],
        "x_scales": packed_xT[1],
        "w1": (n((K, H)) / np.sqrt(K) / s).astype(np.float32),
        "sza": (np.random.uniform(1.0, 3.0, (H, V))).astype(np.float32),
        "szb": (np.random.uniform(1.0, 3.0, (H, V))).astype(np.float32),
        "unit": (np.random.uniform(0.6, 1.4, (H, 1)) * u[:, None]).astype(np.float32),
        "w2": (n((H, N)) / np.sqrt(H) / u[:, None]).astype(np.float32),
        "skip": (n((N, U))).astype(np.float32),
        "offs": striped(np.random.permutation(T)[:S]),
        "dst": striped(np.random.permutation(S)[:V]),
        "src": striped(np.random.permutation(S)[:V]),
        "own": striped(np.random.permutation(np.concatenate([np.arange(V), np.random.randint(0, V, U - V)]))),
    }


def reference(x_words, x_scales, w1, sza, szb, unit, w2, skip, offs, dst, src, own):
    xq = unpack_weight(x_words, x_scales)[:, unstriped(offs)]
    y = mxq(f64(w1), 0, "e4m3").T @ xq
    yd = y[:, unstriped(dst)]
    yr = y[:, unstriped(src)]
    sz = f64(sza) + f64(szb)
    mrg = (yd * f64(sza) + yr * f64(szb)) / sz
    hm = gelu(mrg)
    un = hm[:, unstriped(own)]
    hid = f64(unit) * un
    rr = mxq(f64(w2), 0, "e4m3").T @ mxq(hid, 0, "e4m3")
    return rr + f64(skip)

@@ -1,0 +1,234 @@
+from contextlib import ExitStack
+
+import concourse.mybir as mybir
+from concourse.masks import make_identity
+
+K, T, S, N, H, V, U = 1024, 2048, 512, 128, 512, 256, 512
+FLOPS = 2 * K * H * S + 2 * H * N * U
+
+F32 = mybir.dt.float32
+BF16 = mybir.dt.bfloat16
+I32 = mybir.dt.int32
+U32 = mybir.dt.uint32
+U16 = mybir.dt.uint16
+U8 = mybir.dt.uint8
+FP8X4 = mybir.dt.float8_e4m3fn_x4
+ACT = mybir.ActivationFunctionType
+ALU = mybir.AluOpType
+
+P = 128
+PACK = 4
+PASSES = K // (P * PACK)
+W1_SPLIT = 96
+HALF = S // 2
+
+
+def tile_picked_ytomeg_gelu_p_kernel(
+    tc, x_words, x_scales, w1, sza, szb, unit, w2, skip, offs, dst, src, own, out
+):
+    nc = tc.nc
+    with ExitStack() as ctx:
+        keep = ctx.enter_context(tc.tile_pool(name="keep", bufs=1))
+        psum = ctx.enter_context(tc.psum_pool(name="psum", bufs=1))
+
+        def sb(shape, dtype, name, tag=None):
+            return keep.tile(shape, dtype, name=name, tag=tag or name, align_bytes=64)
+
+        def bank(shape, name, b):
+            return psum.tile(shape, F32, name=name, tag="bank%d" % b)
+
+        offs_sb = keep.tile([P, S // 16], U16, name="offs_sb")
+        dst_sb = keep.tile([P, V // 16], U16, name="dst_sb")
+        src_sb = keep.tile([P, V // 16], U16, name="src_sb")
+        own_sb = keep.tile([P, U // 16], U16, name="own_sb")
+
+        xs_table = sb([P, T], U8, "xs_table")
+        nc.gpsimd.memset(xs_table[:].bitcast(I32), 0)
+        one = sb([P, 1], F32, "one")
+        warm = sb([P, 1], F32, "warm")
+        nc.vector.memset(one[:], 1.0)
+        nc.scalar.activation(warm[:], one[:], ACT.Abs_reciprocal_sqrt)
+        ident = sb([P, P], F32, "ident")
+        make_identity(nc, ident[:])
+        windows = [sb([P, 2 * V], F32, "win%d" % t) for t in range(PACK)]
+        for t in range(PACK):
+            nc.vector.memset(windows[t][:, V:], 0.0)
+
+        w1_raw = [sb([P, PACK, H], F32, "w1_raw%d" % g) for g in range(PASSES)]
+        x_table = [sb([P, T], I32, "x_table%d" % g) for g in range(PASSES)]
+        sza_sb = [sb([P, 2, V], F32, "sza%d" % i) for i in range(2)]
+        szb_sb = [sb([P, 2, V], F32, "szb%d" % i) for i in range(2)]
+        unit_sb = sb([P, PACK], F32, "unit_sb", tag="late")
+        w2_raw = sb([P, PACK, N], F32, "w2_raw")
+        skip_sb = sb([P, U], F32, "skip_sb")
+
+        def load_w1(g):
+            rows = w1[g * P * PACK : (g + 1) * P * PACK, :]
+            nc.sync.dma_start(out=w1_raw[g][:], in_=rows.rearrange("(p j) c -> p j c", j=PACK))
+
+        def load_x(g):
+            nc.sync.dma_start(out=x_table[g][:], in_=x_words[g].rearrange("p n t -> p (n t)").bitcast(I32))
+
+        load_w1(0)
+        for q in range(4):
+            nc.sync.dma_start(
+                out=xs_table[32 * q : 32 * q + 4 * PASSES, :].bitcast(I32),
+                in_=x_scales[:, 4 * q : 4 * q + 4, :].bitcast(I32),
+            )
+        nc.sync.dma_start(offs_sb[:], offs)
+        load_x(0)
+        load_w1(1)
+        load_x(1)
+        nc.sync.dma_start(out=w2_raw[:], in_=w2.rearrange("(p j) n -> p j n", j=PACK))
+        sza_v = sza.rearrange("(p t) v -> p t v", t=PACK)
+        szb_v = szb.rearrange("(p t) v -> p t v", t=PACK)
+        nc.sync.dma_start(dst_sb[:], dst)
+        nc.sync.dma_start(out=sza_sb[0][:], in_=sza_v[:, 0:2, :])
+        nc.sync.dma_start(src_sb[:], src)
+        nc.sync.dma_start(out=szb_sb[0][:], in_=szb_v[:, 0:2, :])
+        nc.sync.dma_start(out=sza_sb[1][:], in_=sza_v[:, 2:4, :])
+        nc.sync.dma_start(out=szb_sb[1][:], in_=szb_v[:, 2:4, :])
+        nc.sync.dma_start(own_sb[:], own)
+        nc.sync.dma_start(out=unit_sb[:], in_=unit.rearrange("(p t) o -> p (t o)", t=PACK))
+        nc.sync.dma_start(out=skip_sb[:], in_=skip)
+
+        xs_picked = sb([P, S], U8, "xs_picked")
+        pieces = [(0, slice(0, HALF)), (0, slice(HALF, S))] + [(t, slice(0, S)) for t in range(1, PACK)]
+        y_ps = [bank([P, c.stop - c.start], "y_ps%d" % b, b) for b, (t, c) in enumerate(pieces)]
+        for g in range(PASSES):
+            grouped = sb([P, H * PACK], BF16, "w1_grouped%d" % g)
+            o = grouped[:].rearrange("p (t m j) -> p m j t", t=PACK, j=PACK)
+            i = w1_raw[g][:].rearrange("p j (m t) -> p m j t", t=PACK)
+            nc.vector.tensor_copy(out=o[:, :W1_SPLIT], in_=i[:, :W1_SPLIT])
+            nc.scalar.copy(out=o[:, W1_SPLIT:], in_=i[:, W1_SPLIT:])
+            w1_codes = sb([P, H], U32, "w1_codes%d" % g)
+            w1_scales = sb([P, H], U8, "w1_scales%d" % g)
+            nc.vector.quantize_mx(out=w1_codes[:].bitcast(FP8X4), scales=w1_scales[:], in_=grouped[:])
+            x_picked = sb([P, S], U32, "x_picked%d" % g)
+            window = x_table[g][:].bitcast(U32)
+            if g == 0:
+                nc.vector.tensor_copy(xs_picked[:], xs_table[:].indirect(offs_sb[:]))
+                nc.vector.tensor_copy(x_picked[:], window.indirect(offs_sb[:]))
+            else:
+                for h in range(2):
+                    nc.vector.tensor_copy(
+                        x_picked[:, h * HALF : (h + 1) * HALF],
+                        window.indirect(offs_sb[:, h * HALF // 16 : (h + 1) * HALF // 16]),
+                    )
+            for b, (t, c) in enumerate(pieces):
+                cols = slice(t * P, (t + 1) * P)
+                nc.tensor.matmul_mx(
+                    out=y_ps[b][:],
+                    lhsT=w1_codes[:, cols].bitcast(FP8X4),
+                    lhsT_scale=w1_scales[:, cols],
+                    rhs=x_picked[:, c].bitcast(FP8X4),
+                    rhs_scale=xs_picked[4 * g : P, c],
+                    start=(g == 0),
+                    stop=(g == PASSES - 1),
+                )
+        y_sb = [sb([P, S], F32, "y_sb%d" % t) for t in range(PACK)]
+        for b, (t, c) in enumerate(pieces):
+            nc.scalar.copy(out=y_sb[t][:, c], in_=y_ps[b][:])
+
+        w2_grouped = sb([P, N * PACK], BF16, "w2_grouped")
+        nc.vector.tensor_copy(
+            out=w2_grouped[:].rearrange("p (c i j) -> p c j i", i=4, j=PACK),
+            in_=w2_raw[:].rearrange("p j (c i) -> p c j i", i=4),
+        )
+        w2_codes = sb([P, N], U32, "w2_codes")
+        w2_scales = sb([P, N], U8, "w2_scales")
+        nc.vector.quantize_mx(out=w2_codes[:].bitcast(FP8X4), scales=w2_scales[:], in_=w2_grouped[:])
+
+        def turned_sum(dest, a, b):
+            for h in range(V // P):
+                cols = slice(h * P, (h + 1) * P)
+                nc.tensor.matmul(dest[:, cols], a[:, cols], ident[:], start=True, stop=False, is_transpose=True)
+                nc.tensor.matmul(dest[:, cols], b[:, cols], ident[:], start=False, stop=True, is_transpose=True)
+
+        recip = []
+        for i in range(2):
+            sz_ps = bank([P, 2, V], "sz_ps%d" % i, 5 + i)
+            for k in range(2):
+                turned_sum(sz_ps[:, k, :], sza_sb[i][:, k, :], szb_sb[i][:, k, :])
+            flat = sz_ps[:].rearrange("p k v -> p (k v)")
+            root = sb([P, 2 * V], F32, "root%d" % i)
+            sgn = sb([P, 2 * V], F32, "sgn%d" % i)
+            mag = sb([P, 2 * V], F32, "mag%d" % i)
+            r = sb([P, 2 * V], F32, "recip%d" % i)
+            nc.scalar.activation(root[:], flat, ACT.Abs_reciprocal_sqrt)
+            nc.scalar.activation(sgn[:], flat, ACT.Sign)
+            nc.scalar.activation(mag[:], root[:], ACT.Square)
+            nc.vector.tensor_tensor(r[:], mag[:], sgn[:], ALU.mult)
+            recip.append(r)
+
+        for t in range(PACK):
+            pa = sb([P, V], F32, "pa%d" % t)
+            pb = sb([P, V], F32, "pb%d" % t)
+            nc.vector.tensor_tensor(pa[:], y_sb[t][:].indirect(dst_sb[:]), sza_sb[t // 2][:, t % 2, :], ALU.mult)
+            nc.vector.tensor_tensor(pb[:], y_sb[t][:].indirect(src_sb[:]), szb_sb[t // 2][:, t % 2, :], ALU.mult)
+            s_ps = bank([P, V], "s_ps%d" % t, t + 1)
+            turned_sum(s_ps[:], pa[:], pb[:])
+            mrg = sb([P, V], F32, "mrg%d" % t)
+            nc.vector.tensor_tensor(mrg[:], s_ps[:], recip[t // 2][:, (t % 2) * V : (t % 2 + 1) * V], ALU.mult)
+            hm = sb([P, V], F32, "hm%d" % t)
+            nc.scalar.activation(hm[:], mrg[:], ACT.Gelu_apprx_tanh)
+            h_ps = bank([P, V], "h_ps%d" % t, 7 * (t % 2))
+            for h in range(V // P):
+                cols = slice(h * P, (h + 1) * P)
+                nc.tensor.transpose(h_ps[:, cols], hm[:, cols], ident[:])
+            nc.scalar.activation(windows[t][:, :V], h_ps[:], ACT.Copy, scale=unit_sb[:, t : t + 1])
+
+        chunks = [(0, 256), (256, 128), (384, 128)]
+
+        def own_slice(c):
+            start, n = chunks[c]
+            return own_sb[:, start // 16 : (start + n) // 16]
+
+        def gather_planes(c, tag):
+            n = chunks[c][1]
+            planes = sb([P, PACK, n], BF16, "planes%d" % c, tag=tag)
+            for t in range(PACK):
+                nc.vector.tensor_copy(planes[:, t, :], windows[t][:].indirect(own_slice(c)))
+            grouped = sb([P, n * PACK], BF16, "hid_grouped%d" % c)
+            nc.scalar.copy(
+                out=grouped[:].rearrange("p (c i t) -> p c t i", i=4, t=PACK),
+                in_=planes[:].rearrange("p t (c i) -> p c t i", i=4),
+            )
+            return grouped
+
+        def gather_grouped(c, tag):
+            grouped = sb([P, chunks[c][1] * PACK], BF16, "hid_grouped%d" % c, tag=tag)
+            for t in range(PACK):
+                nc.vector.tensor_copy(
+                    grouped[:].rearrange("p (n t) -> p n t", t=PACK)[:, :, t], windows[t][:].indirect(own_slice(c))
+                )
+            return grouped
+
+        def project(c, grouped):
+            n = chunks[c][1]
+            codes = sb([P, n], U32, "hid_codes%d" % c)
+            scales = sb([P, n], U8, "hid_scales%d" % c)
+            nc.vector.quantize_mx(out=codes[:].bitcast(FP8X4), scales=scales[:], in_=grouped[:])
+            r_ps = bank([P, n], "r_ps%d" % c, c + 1)
+            nc.tensor.matmul_mx(
+                out=r_ps[:],
+                lhsT=w2_codes[:].bitcast(FP8X4),
+                lhsT_scale=w2_scales[:],
+                rhs=codes[:].bitcast(FP8X4),
+                rhs_scale=scales[:],
+                start=True,
+                stop=True,
+            )
+            return r_ps
+
+        first = gather_planes(0, "first")
+        second = gather_planes(1, "late")
+        products = [project(0, first)]
+        last = gather_grouped(2, "first")
+        products.append(project(1, second))
+        products.append(project(2, last))
+        for c, (start, n) in enumerate(chunks):
+            res = sb([P, n], F32, "res%d" % c)
+            cols = slice(start, start + n)
+            nc.vector.tensor_tensor(res[:], products[c][:], skip_sb[:, cols], ALU.add)
+            nc.sync.dma_start(out=out[:, cols], in_=res[:])

@@ -69,14 +69,18 @@ def tile_picked_ytomeg_gelu_p_kernel(
         def load_x(g):
             nc.sync.dma_start(out=x_table[g][:], in_=x_words[g].rearrange("p n t -> p (n t)").bitcast(I32))
 
+        def load_scale_rows(g):
+            for r in range(4):
+                nc.sync.dma_start(
+                    out=xs_table[4 * g + r : P : 32, :].bitcast(I32),
+                    in_=x_scales[g, r:16:4, :].bitcast(I32),
+                )
+
         load_w1(0)
-        for q in range(4):
-            nc.sync.dma_start(
-                out=xs_table[32 * q : 32 * q + 4 * PASSES, :].bitcast(I32),
-                in_=x_scales[:, 4 * q : 4 * q + 4, :].bitcast(I32),
-            )
-        nc.sync.dma_start(offs_sb[:], offs)
+        load_scale_rows(0)
         load_x(0)
+        nc.sync.dma_start(offs_sb[:], offs)
+        load_scale_rows(1)
         load_w1(1)
         load_x(1)
         nc.sync.dma_start(out=w2_raw[:], in_=w2.rearrange("(p j) n -> p j n", j=PACK))
@@ -92,40 +96,47 @@ def tile_picked_ytomeg_gelu_p_kernel(
         nc.sync.dma_start(out=unit_sb[:], in_=unit.rearrange("(p t) o -> p (t o)", t=PACK))
         nc.sync.dma_start(out=skip_sb[:], in_=skip)
 
-        xs_picked = sb([P, S], U8, "xs_picked")
-        pieces = [(0, slice(0, HALF)), (0, slice(HALF, S))] + [(t, slice(0, S)) for t in range(1, PACK)]
-        y_ps = [bank([P, c.stop - c.start], "y_ps%d" % b, b) for b, (t, c) in enumerate(pieces)]
-        for g in range(PASSES):
+        def quantise_w1(g):
             grouped = sb([P, H * PACK], BF16, "w1_grouped%d" % g)
             o = grouped[:].rearrange("p (t m j) -> p m j t", t=PACK, j=PACK)
             i = w1_raw[g][:].rearrange("p j (m t) -> p m j t", t=PACK)
             nc.vector.tensor_copy(out=o[:, :W1_SPLIT], in_=i[:, :W1_SPLIT])
             nc.scalar.copy(out=o[:, W1_SPLIT:], in_=i[:, W1_SPLIT:])
-            w1_codes = sb([P, H], U32, "w1_codes%d" % g)
-            w1_scales = sb([P, H], U8, "w1_scales%d" % g)
-            nc.vector.quantize_mx(out=w1_codes[:].bitcast(FP8X4), scales=w1_scales[:], in_=grouped[:])
-            x_picked = sb([P, S], U32, "x_picked%d" % g)
-            window = x_table[g][:].bitcast(U32)
-            if g == 0:
-                nc.vector.tensor_copy(xs_picked[:], xs_table[:].indirect(offs_sb[:]))
-                nc.vector.tensor_copy(x_picked[:], window.indirect(offs_sb[:]))
-            else:
-                for h in range(2):
-                    nc.vector.tensor_copy(
-                        x_picked[:, h * HALF : (h + 1) * HALF],
-                        window.indirect(offs_sb[:, h * HALF // 16 : (h + 1) * HALF // 16]),
-                    )
-            for b, (t, c) in enumerate(pieces):
-                cols = slice(t * P, (t + 1) * P)
-                nc.tensor.matmul_mx(
-                    out=y_ps[b][:],
-                    lhsT=w1_codes[:, cols].bitcast(FP8X4),
-                    lhsT_scale=w1_scales[:, cols],
-                    rhs=x_picked[:, c].bitcast(FP8X4),
-                    rhs_scale=xs_picked[4 * g : P, c],
-                    start=(g == 0),
-                    stop=(g == PASSES - 1),
-                )
+            codes = sb([P, H], U32, "w1_codes%d" % g)
+            scales = sb([P, H], U8, "w1_scales%d" % g)
+            nc.vector.quantize_mx(out=codes[:].bitcast(FP8X4), scales=scales[:], in_=grouped[:])
+            w1_codes.append(codes)
+            w1_scales.append(scales)
+
+        w1_codes, w1_scales = [], []
+        xs_picked = sb([P, S], U8, "xs_picked")
+        x_picked = [sb([P, S], U32, "x_picked%d" % g) for g in range(PASSES)]
+        quantise_w1(0)
+        nc.vector.tensor_copy(x_picked[0][:], x_table[0][:].bitcast(U32).indirect(offs_sb[:]))
+        nc.vector.tensor_copy(xs_picked[:], xs_table[:].indirect(offs_sb[:]))
+        quantise_w1(1)
+        for h in range(2):
+            nc.vector.tensor_copy(
+                x_picked[1][:, h * HALF : (h + 1) * HALF],
+                x_table[1][:].bitcast(U32).indirect(offs_sb[:, h * HALF // 16 : (h + 1) * HALF // 16]),
+            )
+
+        pieces = [(0, slice(0, HALF)), (0, slice(HALF, S))] + [(t, slice(0, S)) for t in range(1, PACK)]
+        y_ps = [bank([P, c.stop - c.start], "y_ps%d" % b, b) for b, (t, c) in enumerate(pieces)]
+        for tile in range(PACK):
+            cols = slice(tile * P, (tile + 1) * P)
+            for g in range(PASSES):
+                for b, (t, c) in enumerate(pieces):
+                    if t == tile:
+                        nc.tensor.matmul_mx(
+                            out=y_ps[b][:],
+                            lhsT=w1_codes[g][:, cols].bitcast(FP8X4),
+                            lhsT_scale=w1_scales[g][:, cols],
+                            rhs=x_picked[g][:, c].bitcast(FP8X4),
+                            rhs_scale=xs_picked[4 * g : P, c],
+                            start=(g == 0),
+                            stop=(g == PASSES - 1),
+                        )
         y_sb = [sb([P, S], F32, "y_sb%d" % t) for t in range(PACK)]
         for b, (t, c) in enumerate(pieces):
             nc.scalar.copy(out=y_sb[t][:, c], in_=y_ps[b][:])
@@ -204,9 +215,9 @@ def tile_picked_ytomeg_gelu_p_kernel(
                 )
             return grouped
 
-        def project(c, grouped):
+        def project(c, grouped, tag=None):
             n = chunks[c][1]
-            codes = sb([P, n], U32, "hid_codes%d" % c)
+            codes = sb([P, n], U32, "hid_codes%d" % c, tag=tag)
             scales = sb([P, n], U8, "hid_scales%d" % c)
             nc.vector.quantize_mx(out=codes[:].bitcast(FP8X4), scales=scales[:], in_=grouped[:])
             r_ps = bank([P, n], "r_ps%d" % c, c + 1)
@@ -222,12 +233,13 @@ def tile_picked_ytomeg_gelu_p_kernel(
             return r_ps
 
         first = gather_planes(0, "first")
-        second = gather_planes(1, "late")
-        products = [project(0, first)]
-        last = gather_grouped(2, "first")
-        products.append(project(1, second))
-        products.append(project(2, last))
-        for c, (start, n) in enumerate(chunks):
+        second = gather_planes(1, "second")
+        last = gather_grouped(2, "late")
+        products = {0: project(0, first)}
+        products[2] = project(2, last, "first")
+        products[1] = project(1, second)
+        for c in (0, 2, 1):
+            start, n = chunks[c]
             res = sb([P, n], F32, "res%d" % c)
             cols = slice(start, start + n)
             nc.vector.tensor_tensor(res[:], products[c][:], skip_sb[:, cols], ALU.add)

@@ -19,7 +19,7 @@ ALU = mybir.AluOpType
 P = 128
 PACK = 4
 PASSES = K // (P * PACK)
-W1_SPLIT = 96
+W1_SPLIT = (96, 64)
 HALF = S // 2
 
 
@@ -76,32 +76,61 @@ def tile_picked_ytomeg_gelu_p_kernel(
                     in_=x_scales[g, r:16:4, :].bitcast(I32),
                 )
 
+        sza_v = sza.rearrange("(p t) v -> p t v", t=PACK)
+        szb_v = szb.rearrange("(p t) v -> p t v", t=PACK)
+        for i in range(2):
+            nc.sync.dma_start(out=sza_sb[i][:], in_=sza_v[:, 2 * i : 2 * i + 2, :])
+            nc.sync.dma_start(out=szb_sb[i][:], in_=szb_v[:, 2 * i : 2 * i + 2, :])
+        nc.sync.dma_start(offs_sb[:], offs)
         load_w1(0)
         load_scale_rows(0)
         load_x(0)
-        nc.sync.dma_start(offs_sb[:], offs)
         load_scale_rows(1)
         load_w1(1)
         load_x(1)
         nc.sync.dma_start(out=w2_raw[:], in_=w2.rearrange("(p j) n -> p j n", j=PACK))
-        sza_v = sza.rearrange("(p t) v -> p t v", t=PACK)
-        szb_v = szb.rearrange("(p t) v -> p t v", t=PACK)
         nc.sync.dma_start(dst_sb[:], dst)
-        nc.sync.dma_start(out=sza_sb[0][:], in_=sza_v[:, 0:2, :])
         nc.sync.dma_start(src_sb[:], src)
-        nc.sync.dma_start(out=szb_sb[0][:], in_=szb_v[:, 0:2, :])
-        nc.sync.dma_start(out=sza_sb[1][:], in_=sza_v[:, 2:4, :])
-        nc.sync.dma_start(out=szb_sb[1][:], in_=szb_v[:, 2:4, :])
         nc.sync.dma_start(own_sb[:], own)
         nc.sync.dma_start(out=unit_sb[:], in_=unit.rearrange("(p t) o -> p (t o)", t=PACK))
         nc.sync.dma_start(out=skip_sb[:], in_=skip)
+
+        share_a, share_b = [], []
+        recip = []
+        for i in range(2):
+            total = sb([P, 2 * V], F32, "total%d" % i)
+            root = sb([P, 2 * V], F32, "root%d" % i)
+            sgn = sb([P, 2 * V], F32, "sgn%d" % i)
+            mag = sb([P, 2 * V], F32, "mag%d" % i)
+            nc.vector.tensor_tensor(
+                total[:], sza_sb[i][:].rearrange("p k v -> p (k v)"), szb_sb[i][:].rearrange("p k v -> p (k v)"), ALU.add
+            )
+            nc.scalar.activation(root[:], total[:], ACT.Abs_reciprocal_sqrt)
+            nc.scalar.activation(sgn[:], total[:], ACT.Sign)
+            nc.scalar.activation(mag[:], root[:], ACT.Square)
+            recip.append((mag, sgn))
+
+        def make_shares(i):
+            mag, sgn = recip[i]
+            r = sb([P, 2 * V], F32, "recip%d" % i)
+            a = sb([P, 2 * V], F32, "share_a%d" % i)
+            b = sb([P, 2 * V], F32, "share_b%d" % i)
+            nc.vector.tensor_tensor(r[:], mag[:], sgn[:], ALU.mult)
+            nc.vector.tensor_tensor(a[:], r[:], sza_sb[i][:].rearrange("p k v -> p (k v)"), ALU.mult)
+            nc.scalar.activation(b[:], a[:], ACT.Identity, scale=-1.0, bias=1.0)
+            share_a.append(a)
+            share_b.append(b)
 
         def quantise_w1(g):
             grouped = sb([P, H * PACK], BF16, "w1_grouped%d" % g)
             o = grouped[:].rearrange("p (t m j) -> p m j t", t=PACK, j=PACK)
             i = w1_raw[g][:].rearrange("p j (m t) -> p m j t", t=PACK)
-            nc.vector.tensor_copy(out=o[:, :W1_SPLIT], in_=i[:, :W1_SPLIT])
-            nc.scalar.copy(out=o[:, W1_SPLIT:], in_=i[:, W1_SPLIT:])
+            split = W1_SPLIT[g]
+            nc.vector.tensor_copy(out=o[:, :split], in_=i[:, :split])
+            nc.scalar.copy(out=o[:, split:], in_=i[:, split:])
+            return grouped
+
+        def quantise_grouped(g, grouped):
             codes = sb([P, H], U32, "w1_codes%d" % g)
             scales = sb([P, H], U8, "w1_scales%d" % g)
             nc.vector.quantize_mx(out=codes[:].bitcast(FP8X4), scales=scales[:], in_=grouped[:])
@@ -111,10 +140,17 @@ def tile_picked_ytomeg_gelu_p_kernel(
         w1_codes, w1_scales = [], []
         xs_picked = sb([P, S], U8, "xs_picked")
         x_picked = [sb([P, S], U32, "x_picked%d" % g) for g in range(PASSES)]
-        quantise_w1(0)
+        make_shares(0)
+        first_grouped = quantise_w1(0)
+        warm_gelu = sb([P, 1], F32, "warm_gelu")
+        nc.scalar.activation(
+            warm_gelu[:], first_grouped[:, H * PACK - 1 :], ACT.Gelu_apprx_tanh, bias=recip[1][0][:, 0:1]
+        )
+        make_shares(1)
+        quantise_grouped(0, first_grouped)
         nc.vector.tensor_copy(x_picked[0][:], x_table[0][:].bitcast(U32).indirect(offs_sb[:]))
         nc.vector.tensor_copy(xs_picked[:], xs_table[:].indirect(offs_sb[:]))
-        quantise_w1(1)
+        quantise_grouped(1, quantise_w1(1))
         for h in range(2):
             nc.vector.tensor_copy(
                 x_picked[1][:, h * HALF : (h + 1) * HALF],
@@ -156,33 +192,16 @@ def tile_picked_ytomeg_gelu_p_kernel(
                 nc.tensor.matmul(dest[:, cols], a[:, cols], ident[:], start=True, stop=False, is_transpose=True)
                 nc.tensor.matmul(dest[:, cols], b[:, cols], ident[:], start=False, stop=True, is_transpose=True)
 
-        recip = []
-        for i in range(2):
-            sz_ps = bank([P, 2, V], "sz_ps%d" % i, 5 + i)
-            for k in range(2):
-                turned_sum(sz_ps[:, k, :], sza_sb[i][:, k, :], szb_sb[i][:, k, :])
-            flat = sz_ps[:].rearrange("p k v -> p (k v)")
-            root = sb([P, 2 * V], F32, "root%d" % i)
-            sgn = sb([P, 2 * V], F32, "sgn%d" % i)
-            mag = sb([P, 2 * V], F32, "mag%d" % i)
-            r = sb([P, 2 * V], F32, "recip%d" % i)
-            nc.scalar.activation(root[:], flat, ACT.Abs_reciprocal_sqrt)
-            nc.scalar.activation(sgn[:], flat, ACT.Sign)
-            nc.scalar.activation(mag[:], root[:], ACT.Square)
-            nc.vector.tensor_tensor(r[:], mag[:], sgn[:], ALU.mult)
-            recip.append(r)
-
         for t in range(PACK):
             pa = sb([P, V], F32, "pa%d" % t)
             pb = sb([P, V], F32, "pb%d" % t)
-            nc.vector.tensor_tensor(pa[:], y_sb[t][:].indirect(dst_sb[:]), sza_sb[t // 2][:, t % 2, :], ALU.mult)
-            nc.vector.tensor_tensor(pb[:], y_sb[t][:].indirect(src_sb[:]), szb_sb[t // 2][:, t % 2, :], ALU.mult)
-            s_ps = bank([P, V], "s_ps%d" % t, t + 1)
+            pairs = slice((t % 2) * V, (t % 2 + 1) * V)
+            nc.vector.tensor_tensor(pa[:], y_sb[t][:].indirect(dst_sb[:]), share_a[t // 2][:, pairs], ALU.mult)
+            nc.vector.tensor_tensor(pb[:], y_sb[t][:].indirect(src_sb[:]), share_b[t // 2][:, pairs], ALU.mult)
+            s_ps = bank([P, V], "s_ps%d" % t, 5 + t % 2)
             turned_sum(s_ps[:], pa[:], pb[:])
-            mrg = sb([P, V], F32, "mrg%d" % t)
-            nc.vector.tensor_tensor(mrg[:], s_ps[:], recip[t // 2][:, (t % 2) * V : (t % 2 + 1) * V], ALU.mult)
             hm = sb([P, V], F32, "hm%d" % t)
-            nc.scalar.activation(hm[:], mrg[:], ACT.Gelu_apprx_tanh)
+            nc.scalar.activation(hm[:], s_ps[:], ACT.Gelu_apprx_tanh)
             h_ps = bank([P, V], "h_ps%d" % t, 7 * (t % 2))
             for h in range(V // P):
                 cols = slice(h * P, (h + 1) * P)

from contextlib import ExitStack

import concourse.mybir as mybir
from concourse.masks import make_identity

K, T, S, N, H, V, U = 1024, 2048, 512, 128, 512, 256, 512
FLOPS = 2 * K * H * S + 2 * H * N * U

F32 = mybir.dt.float32
BF16 = mybir.dt.bfloat16
I32 = mybir.dt.int32
U32 = mybir.dt.uint32
U16 = mybir.dt.uint16
U8 = mybir.dt.uint8
FP8X4 = mybir.dt.float8_e4m3fn_x4
ACT = mybir.ActivationFunctionType
ALU = mybir.AluOpType

P = 128
PACK = 4
PASSES = K // (P * PACK)
W1_SPLIT = (96, 64)
HALF = S // 2


def tile_picked_ytomeg_gelu_p_kernel(
    tc, x_words, x_scales, w1, sza, szb, unit, w2, skip, offs, dst, src, own, out
):
    nc = tc.nc
    with ExitStack() as ctx:
        keep = ctx.enter_context(tc.tile_pool(name="keep", bufs=1))
        psum = ctx.enter_context(tc.psum_pool(name="psum", bufs=1))

        def sb(shape, dtype, name, tag=None):
            return keep.tile(shape, dtype, name=name, tag=tag or name, align_bytes=64)

        def bank(shape, name, b):
            return psum.tile(shape, F32, name=name, tag="bank%d" % b)

        offs_sb = keep.tile([P, S // 16], U16, name="offs_sb")
        dst_sb = keep.tile([P, V // 16], U16, name="dst_sb")
        src_sb = keep.tile([P, V // 16], U16, name="src_sb")
        own_sb = keep.tile([P, U // 16], U16, name="own_sb")

        xs_table = sb([P, T], U8, "xs_table")
        nc.gpsimd.memset(xs_table[:].bitcast(I32), 0)
        one = sb([P, 1], F32, "one")
        warm = sb([P, 1], F32, "warm")
        nc.vector.memset(one[:], 1.0)
        nc.scalar.activation(warm[:], one[:], ACT.Abs_reciprocal_sqrt)
        ident = sb([P, P], F32, "ident")
        make_identity(nc, ident[:])
        windows = [sb([P, 2 * V], F32, "win%d" % t) for t in range(PACK)]
        for t in range(PACK):
            nc.vector.memset(windows[t][:, V:], 0.0)

        w1_raw = [sb([P, PACK, H], F32, "w1_raw%d" % g) for g in range(PASSES)]
        x_table = [sb([P, T], I32, "x_table%d" % g) for g in range(PASSES)]
        sza_sb = [sb([P, 2, V], F32, "sza%d" % i) for i in range(2)]
        szb_sb = [sb([P, 2, V], F32, "szb%d" % i) for i in range(2)]
        unit_sb = sb([P, PACK], F32, "unit_sb", tag="late")
        w2_raw = sb([P, PACK, N], F32, "w2_raw")
        skip_sb = sb([P, U], F32, "skip_sb")

        def load_w1(g):
            rows = w1[g * P * PACK : (g + 1) * P * PACK, :]
            nc.sync.dma_start(out=w1_raw[g][:], in_=rows.rearrange("(p j) c -> p j c", j=PACK))

        def load_x(g):
            nc.sync.dma_start(out=x_table[g][:], in_=x_words[g].rearrange("p n t -> p (n t)").bitcast(I32))

        def load_scale_rows(g):
            for r in range(4):
                nc.sync.dma_start(
                    out=xs_table[4 * g + r : P : 32, :].bitcast(I32),
                    in_=x_scales[g, r:16:4, :].bitcast(I32),
                )

        sza_v = sza.rearrange("(p t) v -> p t v", t=PACK)
        szb_v = szb.rearrange("(p t) v -> p t v", t=PACK)
        for i in range(2):
            nc.sync.dma_start(out=sza_sb[i][:], in_=sza_v[:, 2 * i : 2 * i + 2, :])
            nc.sync.dma_start(out=szb_sb[i][:], in_=szb_v[:, 2 * i : 2 * i + 2, :])
        nc.sync.dma_start(offs_sb[:], offs)
        load_w1(0)
        load_scale_rows(0)
        load_x(0)
        load_scale_rows(1)
        load_w1(1)
        load_x(1)
        nc.sync.dma_start(out=w2_raw[:], in_=w2.rearrange("(p j) n -> p j n", j=PACK))
        nc.sync.dma_start(dst_sb[:], dst)
        nc.sync.dma_start(src_sb[:], src)
        nc.sync.dma_start(own_sb[:], own)
        nc.sync.dma_start(out=unit_sb[:], in_=unit.rearrange("(p t) o -> p (t o)", t=PACK))
        nc.sync.dma_start(out=skip_sb[:], in_=skip)

        share_a, share_b = [], []
        recip = []
        for i in range(2):
            total = sb([P, 2 * V], F32, "total%d" % i)
            root = sb([P, 2 * V], F32, "root%d" % i)
            sgn = sb([P, 2 * V], F32, "sgn%d" % i)
            mag = sb([P, 2 * V], F32, "mag%d" % i)
            nc.vector.tensor_tensor(
                total[:], sza_sb[i][:].rearrange("p k v -> p (k v)"), szb_sb[i][:].rearrange("p k v -> p (k v)"), ALU.add
            )
            nc.scalar.activation(root[:], total[:], ACT.Abs_reciprocal_sqrt)
            nc.scalar.activation(sgn[:], total[:], ACT.Sign)
            nc.scalar.activation(mag[:], root[:], ACT.Square)
            recip.append((mag, sgn))

        def make_shares(i):
            mag, sgn = recip[i]
            r = sb([P, 2 * V], F32, "recip%d" % i)
            a = sb([P, 2 * V], F32, "share_a%d" % i)
            b = sb([P, 2 * V], F32, "share_b%d" % i)
            nc.vector.tensor_tensor(r[:], mag[:], sgn[:], ALU.mult)
            nc.vector.tensor_tensor(a[:], r[:], sza_sb[i][:].rearrange("p k v -> p (k v)"), ALU.mult)
            nc.scalar.activation(b[:], a[:], ACT.Identity, scale=-1.0, bias=1.0)
            share_a.append(a)
            share_b.append(b)

        def quantise_w1(g):
            grouped = sb([P, H * PACK], BF16, "w1_grouped%d" % g)
            o = grouped[:].rearrange("p (t m j) -> p m j t", t=PACK, j=PACK)
            i = w1_raw[g][:].rearrange("p j (m t) -> p m j t", t=PACK)
            split = W1_SPLIT[g]
            nc.vector.tensor_copy(out=o[:, :split], in_=i[:, :split])
            nc.scalar.copy(out=o[:, split:], in_=i[:, split:])
            return grouped

        def quantise_grouped(g, grouped):
            codes = sb([P, H], U32, "w1_codes%d" % g)
            scales = sb([P, H], U8, "w1_scales%d" % g)
            nc.vector.quantize_mx(out=codes[:].bitcast(FP8X4), scales=scales[:], in_=grouped[:])
            w1_codes.append(codes)
            w1_scales.append(scales)

        w1_codes, w1_scales = [], []
        xs_picked = sb([P, S], U8, "xs_picked")
        x_picked = [sb([P, S], U32, "x_picked%d" % g) for g in range(PASSES)]
        make_shares(0)
        first_grouped = quantise_w1(0)
        warm_gelu = sb([P, 1], F32, "warm_gelu")
        nc.scalar.activation(
            warm_gelu[:], first_grouped[:, H * PACK - 1 :], ACT.Gelu_apprx_tanh, bias=recip[1][0][:, 0:1]
        )
        make_shares(1)
        quantise_grouped(0, first_grouped)
        nc.vector.tensor_copy(x_picked[0][:], x_table[0][:].bitcast(U32).indirect(offs_sb[:]))
        nc.vector.tensor_copy(xs_picked[:], xs_table[:].indirect(offs_sb[:]))
        quantise_grouped(1, quantise_w1(1))
        for h in range(2):
            nc.vector.tensor_copy(
                x_picked[1][:, h * HALF : (h + 1) * HALF],
                x_table[1][:].bitcast(U32).indirect(offs_sb[:, h * HALF // 16 : (h + 1) * HALF // 16]),
            )

        pieces = [(0, slice(0, HALF)), (0, slice(HALF, S))] + [(t, slice(0, S)) for t in range(1, PACK)]
        y_ps = [bank([P, c.stop - c.start], "y_ps%d" % b, b) for b, (t, c) in enumerate(pieces)]
        for tile in range(PACK):
            cols = slice(tile * P, (tile + 1) * P)
            for g in range(PASSES):
                for b, (t, c) in enumerate(pieces):
                    if t == tile:
                        nc.tensor.matmul_mx(
                            out=y_ps[b][:],
                            lhsT=w1_codes[g][:, cols].bitcast(FP8X4),
                            lhsT_scale=w1_scales[g][:, cols],
                            rhs=x_picked[g][:, c].bitcast(FP8X4),
                            rhs_scale=xs_picked[4 * g : P, c],
                            start=(g == 0),
                            stop=(g == PASSES - 1),
                        )
        y_sb = [sb([P, S], F32, "y_sb%d" % t) for t in range(PACK)]
        for b, (t, c) in enumerate(pieces):
            nc.scalar.copy(out=y_sb[t][:, c], in_=y_ps[b][:])

        w2_grouped = sb([P, N * PACK], BF16, "w2_grouped")
        nc.vector.tensor_copy(
            out=w2_grouped[:].rearrange("p (c i j) -> p c j i", i=4, j=PACK),
            in_=w2_raw[:].rearrange("p j (c i) -> p c j i", i=4),
        )
        w2_codes = sb([P, N], U32, "w2_codes")
        w2_scales = sb([P, N], U8, "w2_scales")
        nc.vector.quantize_mx(out=w2_codes[:].bitcast(FP8X4), scales=w2_scales[:], in_=w2_grouped[:])

        def turned_sum(dest, a, b):
            for h in range(V // P):
                cols = slice(h * P, (h + 1) * P)
                nc.tensor.matmul(dest[:, cols], a[:, cols], ident[:], start=True, stop=False, is_transpose=True)
                nc.tensor.matmul(dest[:, cols], b[:, cols], ident[:], start=False, stop=True, is_transpose=True)

        for t in range(PACK):
            pa = sb([P, V], F32, "pa%d" % t)
            pb = sb([P, V], F32, "pb%d" % t)
            pairs = slice((t % 2) * V, (t % 2 + 1) * V)
            nc.vector.tensor_tensor(pa[:], y_sb[t][:].indirect(dst_sb[:]), share_a[t // 2][:, pairs], ALU.mult)
            nc.vector.tensor_tensor(pb[:], y_sb[t][:].indirect(src_sb[:]), share_b[t // 2][:, pairs], ALU.mult)
            s_ps = bank([P, V], "s_ps%d" % t, 5 + t % 2)
            turned_sum(s_ps[:], pa[:], pb[:])
            hm = sb([P, V], F32, "hm%d" % t)
            nc.scalar.activation(hm[:], s_ps[:], ACT.Gelu_apprx_tanh)
            h_ps = bank([P, V], "h_ps%d" % t, 7 * (t % 2))
            for h in range(V // P):
                cols = slice(h * P, (h + 1) * P)
                nc.tensor.transpose(h_ps[:, cols], hm[:, cols], ident[:])
            nc.scalar.activation(windows[t][:, :V], h_ps[:], ACT.Copy, scale=unit_sb[:, t : t + 1])

        chunks = [(0, 256), (256, 128), (384, 128)]

        def own_slice(c):
            start, n = chunks[c]
            return own_sb[:, start // 16 : (start + n) // 16]

        def gather_planes(c, tag):
            n = chunks[c][1]
            planes = sb([P, PACK, n], BF16, "planes%d" % c, tag=tag)
            for t in range(PACK):
                nc.vector.tensor_copy(planes[:, t, :], windows[t][:].indirect(own_slice(c)))
            grouped = sb([P, n * PACK], BF16, "hid_grouped%d" % c)
            nc.scalar.copy(
                out=grouped[:].rearrange("p (c i t) -> p c t i", i=4, t=PACK),
                in_=planes[:].rearrange("p t (c i) -> p c t i", i=4),
            )
            return grouped

        def gather_grouped(c, tag):
            grouped = sb([P, chunks[c][1] * PACK], BF16, "hid_grouped%d" % c, tag=tag)
            for t in range(PACK):
                nc.vector.tensor_copy(
                    grouped[:].rearrange("p (n t) -> p n t", t=PACK)[:, :, t], windows[t][:].indirect(own_slice(c))
                )
            return grouped

        def project(c, grouped, tag=None):
            n = chunks[c][1]
            codes = sb([P, n], U32, "hid_codes%d" % c, tag=tag)
            scales = sb([P, n], U8, "hid_scales%d" % c)
            nc.vector.quantize_mx(out=codes[:].bitcast(FP8X4), scales=scales[:], in_=grouped[:])
            r_ps = bank([P, n], "r_ps%d" % c, c + 1)
            nc.tensor.matmul_mx(
                out=r_ps[:],
                lhsT=w2_codes[:].bitcast(FP8X4),
                lhsT_scale=w2_scales[:],
                rhs=codes[:].bitcast(FP8X4),
                rhs_scale=scales[:],
                start=True,
                stop=True,
            )
            return r_ps

        first = gather_planes(0, "first")
        second = gather_planes(1, "second")
        last = gather_grouped(2, "late")
        products = {0: project(0, first)}
        products[2] = project(2, last, "first")
        products[1] = project(1, second)
        for c in (0, 2, 1):
            start, n = chunks[c]
            res = sb([P, n], F32, "res%d" % c)
            cols = slice(start, start + n)
            nc.vector.tensor_tensor(res[:], products[c][:], skip_sb[:, cols], ALU.add)
            nc.sync.dma_start(out=out[:, cols], in_=res[:])
